import numpy as np, ml_dtypes
CORES = [19,147,275,403]
N = 4
R, TK = 64, 16
def setup_inputs(rng):
    u = (rng.standard_normal((N, 128, R), dtype=np.float32) / 11).astype(ml_dtypes.bfloat16)
    return {"x": rng.standard_normal((N, 128, TK), dtype=np.float32).astype(ml_dtypes.bfloat16), "u": u, "ut": u.transpose(0, 2, 1).copy(), "vt": rng.standard_normal((N, R, 128), dtype=np.float32).astype(ml_dtypes.bfloat16)}
def setup_inputs_big(rng):
    d = setup_inputs(rng)
    for k in ("x", "u", "ut", "vt"): d[k] = (d[k].astype(np.float32) * 1024.0).astype(d[k].dtype)
    return d
def setup_inputs_small(rng):
    d = setup_inputs(rng)
    for k in ("x", "u", "ut", "vt"): d[k] = (d[k].astype(np.float32) * (1 / 1024.0)).astype(d[k].dtype)
    return d
def setup_inputs_apart(rng):
    d = setup_inputs(rng)
    f = (10.0 ** rng.permutation(np.linspace(-1.5, 1.5, N))).astype(np.float32).reshape(N, 1, 1)
    for k in ("x", "u", "ut", "vt"): d[k] = (d[k].astype(np.float32) * f).astype(d[k].dtype)
    return d
def reference(x, u, ut, vt):
    X, U, VT = x.astype(np.float64), u.astype(np.float64), vt.astype(np.float64)
    y = np.stack([sum(VT[j].T @ (U[j].T @ X[r]) for j in range(N)) for r in range(N)])
    return {"y": y.astype(ml_dtypes.bfloat16)}

from concourse.mybir import dt, AluOpType

SCRATCH = {
    "xx": ("sbuf", [128, 32], "bfloat16"),
    "uts": ("sbuf", [64, 128], "bfloat16"),
    "vts": ("sbuf", [64, 128], "bfloat16"),
    "wo": ("sbuf", [128, 128], "bfloat16"),
    "wp": ("sbuf", [128, 128], "bfloat16"),
    "zs": ("sbuf", [128, 16], "bfloat16"),
    "zr": ("sbuf", [128, 16], "bfloat16"),
    "ys": ("sbuf", [128, 16], "bfloat16"),
    "pw": ("psum", [128, 128], "float32"),
    "pzy": ("psum", [128, 32], "float32"),
}
SEMAPHORES = ["ld_x", "ld_uv", "mm_w", "cp_w", "in_x", "in_w", "mm_zy", "cp_z", "in_z", "add_y", "left", "stored"]


def rank_program(g, core, T, topo):
    if T.rank_of(core) is None:
        return
    S = T.sem
    others = [d for d in T.cores if d != core and topo.may_write(core, d)]
    near = [d for d in others if topo.same_plane(core, d)][0]
    far = [d for d in others if topo.rack(topo.host(d)) != topo.rack(topo.host(core))][0]

    def send(dst, out_ap, in_ap, sem):
        rid, pid = topo.addr(dst, core)
        m = topo.mask(core, dst)
        g.remote_dma(out_ap, in_ap, sem, S.left, pid, rid, m)
        return bin(m).count("1")

    n_near = bin(topo.mask(near, core)).count("1")
    n_far = bin(topo.mask(far, core)).count("1")

    g.sync.dma_start(T.xx[:, 0:16], T.x[:, :]).then_inc(S.ld_x, 16)
    g.scalar.dma_start(T.uts[:, :], T.ut[:, :]).then_inc(S.ld_uv, 16)
    g.sync.dma_start(T.vts[:, :], T.vt[:, :]).then_inc(S.ld_uv, 16)

    g.wait_ge(S.ld_x, 16)
    left = send(far, T.xx[:, 16:32], T.xx[:, 0:16], S.in_x)

    g.tensor.wait_ge(S.ld_uv, 32)
    g.tensor.matmul(T.pw[:, :], T.uts[:, :], T.vts[:, :], True, True).then_inc(S.mm_w, 1)
    g.vector.wait_ge(S.mm_w, 1)
    g.vector.tensor_copy(T.wo[:, :], T.pw[:, :]).then_inc(S.cp_w, 1)

    g.wait_ge(S.cp_w, 1)
    left += send(near, T.wp[:, :], T.wo[:, :], S.in_w)

    g.tensor.wait_ge(S.cp_w, 1)
    g.tensor.wait_ge(S.ld_x, 16)
    g.tensor.wait_ge(S.in_x, n_far)
    g.tensor.matmul(T.pzy[:, :], T.wo[:, :], T.xx[:, :], True, False)
    g.tensor.wait_ge(S.in_w, n_near)
    g.tensor.matmul(T.pzy[:, :], T.wp[:, :], T.xx[:, :], False, True).then_inc(S.mm_zy, 1)

    g.vector.wait_ge(S.mm_zy, 1)
    g.vector.tensor_copy(T.zs[:, :], T.pzy[:, 16:32]).then_inc(S.cp_z, 1)
    g.wait_ge(S.cp_z, 1)
    left += send(far, T.zr[:, :], T.zs[:, :], S.in_z)

    g.vector.wait_ge(S.in_z, n_far)
    g.vector.tensor_tensor(T.ys[:, :], T.pzy[:, 0:16], T.zr[:, :], AluOpType.add).then_inc(S.add_y, 1)
    g.sync.wait_ge(S.add_y, 1)
    g.sync.dma_start(T.y[:, :], T.ys[:, :]).then_inc(S.stored, 16)
    g.sync.wait_ge(S.stored, 16)
    g.wait_ge(S.left, left)
